import numpy as np
import ml_dtypes


def mxq(x, axis, fmt="e4m3"):
    dtype, down = {"e4m3": (ml_dtypes.float8_e4m3fn, 7), "e5m2": (ml_dtypes.float8_e5m2, 14)}[fmt]
    v = np.moveaxis(np.asarray(x, np.float32).astype(ml_dtypes.bfloat16).astype(np.float64), axis, -1)
    blocks = v.reshape(v.shape[:-1] + (-1, 32))
    amax = np.abs(blocks).max(-1, keepdims=True)
    byte = np.maximum(np.where(amax > 0, np.frexp(amax)[1] - 1 + 127, 0) - down, 1)
    scale = np.exp2(byte - 127.0)
    codes = (blocks / scale).astype(np.float32).astype(dtype).astype(np.float64)
    return np.moveaxis((codes * scale).reshape(v.shape), -1, axis)


WIDE = False


def mx_kscale(k):
    if not WIDE:
        return np.ones(k)
    levels = np.array([10, -10, 5, -5, 0])
    if k % 512:
        return np.exp2(np.random.permutation(np.resize(levels, k // 32))).repeat(32)
    a = np.empty((k // 512, 16))
    for p in range(k // 512):
        a[p, :8] = np.random.permutation(np.resize(levels, 8))
        for g in range(8):
            far = levels[np.abs(levels - a[p, g]) >= 10]
            a[p, g + 8] = far[np.random.randint(len(far))]
    return np.exp2(a.ravel()).repeat(32)


def f64(x):
    return np.asarray(x).astype(np.float64)


def striped8(idx):
    return np.asarray(idx).reshape(8, -1, 16).transpose(0, 2, 1).reshape(128, -1).astype(np.uint16)


def unstriped8(offs):
    return offs.reshape(8, 16, -1).transpose(0, 2, 1).reshape(8, -1).astype(np.int64)


def pick8(x, idx, run):
    r = np.arange(len(x))
    return x[r[:, None], idx[r % (8 * run) // run]]


E2M1 = np.array([0.0, 0.5, 1.0, 1.5, 2.0, 3.0, 4.0, 6.0, -0.0, -0.5, -1.0, -1.5, -2.0, -3.0, -4.0, -6.0])


def pack_weight(w, fmt):
    k, n = w.shape
    w = f64(np.asarray(w, np.float32).astype(ml_dtypes.bfloat16)).reshape(k // 32, 32, n)
    amax = np.abs(w).max(1)
    if fmt == "e4m3":
        byte = np.frexp(amax)[1] - 1 + 127 - 7
    else:
        mant, ex = np.frexp(amax / 6.0)
        byte = np.where(mant > 0.5, ex, ex - 1) + 127
    byte = np.clip(np.where(amax > 0, byte, 1), 1, 254)
    scaled = (w * np.exp2(127.0 - byte)[:, None, :]).reshape(k, n).astype(np.float32)
    by_word = np.ascontiguousarray(scaled.reshape(k // 512, 128, 4, n).transpose(0, 1, 3, 2))
    if fmt == "e4m3":
        words = by_word.astype(ml_dtypes.float8_e4m3fn).view(np.uint8)
    else:
        c = by_word.astype(ml_dtypes.float4_e2m1fn).view(np.uint8) & 0xF
        words = (c[..., 0::2] | (c[..., 1::2] << 4)).reshape(k // 512, 128, 2 * n)
    return np.ascontiguousarray(words), np.ascontiguousarray(byte.astype(np.uint8).reshape(k // 512, 16, n))


def unpack_weight(words, scales, fmt):
    g, _, n = scales.shape
    words = np.ascontiguousarray(words).reshape(g, 128, n, -1)
    if fmt == "e4m3":
        vals = words.view(ml_dtypes.float8_e4m3fn).astype(np.float64)
    else:
        nib = np.empty((g, 128, n, 4), np.uint8)
        nib[..., 0::2] = words & 0xF
        nib[..., 1::2] = words >> 4
        vals = E2M1[nib]
    vals = vals * np.repeat(np.exp2(scales.astype(np.float64) - 127.0), 8, axis=1)[..., None]
    return vals.transpose(0, 1, 3, 2).reshape(g * 512, n)


D, T, I, Q, G = 512, 1024, 512, 128, 64


def setup_inputs():
    n = np.random.standard_normal
    idx = np.stack([np.random.permutation(T)[:I] for _ in range(8)])
    idx2 = np.stack([np.random.permutation(T)[:I] for _ in range(8)])
    fd = mx_kscale(D)
    keysp = pack_weight(n((D, T)) / fd[:, None], "e2m1")
    return {
        "query": (n((D, Q)) * 0.9 / np.sqrt(D) * fd[:, None]).astype(np.float32),
        "query2": (n((D, Q)) * 0.9 / np.sqrt(D) * fd[:, None]).astype(np.float32),
        "keys_words": keysp[0],
        "keys_scales": keysp[1],
        "lam": (np.random.uniform(0.8, 1.6, (Q, 1))).astype(np.float32),
        "reserve": (np.random.uniform(20.0, 60.0, (Q, 1))).astype(np.float32),
        "old": (np.random.uniform(0.0, 2.0, (Q, T))).astype(np.float32),
        "fade": (np.random.uniform(0.3, 0.9, (Q, 1))).astype(np.float32),
        "offs": striped8(idx),
        "offs2": striped8(idx2),
    }


def reference(query, query2, keys_words, keys_scales, lam, reserve, old, fade, offs, offs2):
    idx = unstriped8(offs)
    idx2 = unstriped8(offs2)
    keysu = unpack_weight(keys_words, keys_scales, "e2m1")
    queryq = mxq(f64(query), 0, "e4m3")
    a = queryq.T @ keysu
    query2q = mxq(f64(query2), 0, "e4m3")
    b = query2q.T @ keysu
    s = np.log(np.exp(pick8(a, idx, 16)) + np.exp(pick8(b, idx2, 16))) * f64(lam)
    p = np.exp(s)
    pg = p.reshape(Q, G, I // G).sum(axis=2)
    pr = np.repeat(pg, I // G, axis=1)
    r = p / (pr - p)
    w = r / (np.sum(r, axis=1, keepdims=True) + f64(reserve))
    ws = w * 256.0
    wf = np.zeros((Q, T))
    wf[np.arange(Q)[:, None], idx[np.arange(Q) % 128 // 16]] = ws
    y = f64(old) * f64(fade) + wf
    return y

@@ -1,0 +1,183 @@
+import math
+from contextlib import ExitStack
+
+import concourse.mybir as mybir
+
+D, T, SLOTS, Q, RUN = 512, 1024, 512, 128, 8
+FLOPS = 2 * 2 * D * Q * T
+
+F32 = mybir.dt.float32
+BF16 = mybir.dt.bfloat16
+I32 = mybir.dt.int32
+U32 = mybir.dt.uint32
+U16 = mybir.dt.uint16
+U8 = mybir.dt.uint8
+FP8X4 = mybir.dt.float8_e4m3fn_x4
+FP4X4 = mybir.dt.float4_e2m1fn_x4
+ALU = mybir.AluOpType
+ACT = mybir.ActivationFunctionType
+AX = mybir.AxisListType
+
+P = 128
+PACK = 4
+PASS_N = 256
+HALF = SLOTS // 2
+QUARTER = SLOTS // 4
+LIST_COLS = SLOTS // 16
+CAP_BITS = 60
+CAP = 2.0**CAP_BITS
+LOG_CAP = CAP_BITS * math.log(2.0)
+OUT_PIECES = [384, 384, 256]
+
+
+def tile_attend_eithertoken_oddsof_counts_heads_kernel(
+    tc, query, query2, keys_words, keys_scales, lam, reserve, old, fade, offs, offs2, out
+):
+    nc = tc.nc
+    with ExitStack() as ctx:
+        pool = ctx.enter_context(tc.tile_pool(name="pool", bufs=1))
+        psum = ctx.enter_context(tc.psum_pool(name="psum", bufs=1))
+
+        def tile(name, shape, dtype=F32):
+            return pool.tile(shape, dtype, name=name, align_bytes=64)
+
+        def half(t, h):
+            return t[:, h * HALF : (h + 1) * HALF]
+
+        def cross(t, c):
+            return t[:].rearrange("p (h c n) -> p h c n", h=2, c=2)[:, :, c, :]
+
+        def runs(ap):
+            return ap.rearrange("p (g e) -> p g e", e=RUN)
+
+        key_scales = tile("key_scales", [P, T], U8)
+        nc.vector.memset(key_scales[:].bitcast(I32), 0)
+        for quad in range(4):
+            nc.scalar.dma_start(
+                out=key_scales[32 * quad : 32 * quad + 4, :].bitcast(I32),
+                in_=keys_scales[0, 4 * quad : 4 * quad + 4, :].bitcast(I32),
+            )
+        q_raw = [tile("q_raw%d" % i, [P, PACK, Q]) for i in range(2)]
+        key_words = tile("key_words", [P, 2 * T], U8)
+        nc.sync.dma_start(out=q_raw[0][:], in_=query.rearrange("(p j) w -> p j w", j=PACK))
+        nc.sync.dma_start(out=key_words[:].bitcast(I32), in_=keys_words[0].bitcast(I32))
+        nc.sync.dma_start(out=q_raw[1][:], in_=query2.rearrange("(p j) w -> p j w", j=PACK))
+        list_a = pool.tile([P, LIST_COLS], U16, name="list_a")
+        list_b = pool.tile([P, LIST_COLS], U16, name="list_b")
+        nc.sync.dma_start(list_a[:], offs)
+        nc.sync.dma_start(list_b[:], offs2)
+        lam_sb = tile("lam_sb", [P, 1])
+        prob = tile("prob", [P, SLOTS + 1])
+        fade_sb = tile("fade_sb", [P, 1])
+        nc.sync.dma_start(out=lam_sb[:], in_=lam)
+        nc.sync.dma_start(out=prob[:, SLOTS : SLOTS + 1], in_=reserve)
+        nc.sync.dma_start(out=fade_sb[:], in_=fade)
+        old_sb = tile("old_sb", [P, T])
+        nc.sync.dma_start(out=old_sb[:], in_=old)
+
+        placed = tile("placed", [P, T])
+        nc.gpsimd.memset(placed[:], 0.0)
+
+        scores = [tile("scores%d" % i, [P, T]) for i in range(2)]
+        for i in range(2):
+            grouped = tile("grouped%d" % i, [P, Q, PACK], BF16)
+            codes = tile("codes%d" % i, [P, Q], U32)
+            q_scales = tile("q_scales%d" % i, [P, Q], U8)
+            nc.vector.tensor_copy(out=grouped[:], in_=q_raw[i][:].rearrange("p j w -> p w j"))
+            nc.vector.quantize_mx(
+                out=codes[:].bitcast(FP8X4), scales=q_scales[:], in_=grouped[:].rearrange("p w j -> p (w j)")
+            )
+            for n0 in range(0, T, PASS_N):
+                bank = psum.tile([Q, PASS_N], F32, name="bank%d_%d" % (i, n0))
+                nc.tensor.matmul_mx(
+                    out=bank[:],
+                    lhsT=codes[:].bitcast(FP8X4),
+                    lhsT_scale=q_scales[:],
+                    rhs=key_words[:, 2 * n0 : 2 * (n0 + PASS_N)].bitcast(FP4X4),
+                    rhs_scale=key_scales[:, n0 : n0 + PASS_N],
+                    start=True,
+                    stop=True,
+                )
+                nc.scalar.copy(out=scores[i][:, n0 : n0 + PASS_N], in_=bank[:])
+
+        def offsets(lst, h):
+            return lst[:, h * LIST_COLS // 2 : (h + 1) * LIST_COLS // 2]
+
+        picked_a = tile("picked_a", [P, SLOTS])
+        nc.vector.tensor_copy(picked_a[:], scores[0][:].indirect(list_a[:]))
+        gap = [tile("gap%d" % h, [P, HALF]) for h in range(2)]
+        picked_b1 = tile("picked_b1", [P, HALF])
+        nc.scalar.activation(picked_b1[:], scores[1][:].indirect(offsets(list_b, 1)), ACT.Copy)
+        nc.vector.tensor_tensor(gap[0][:], scores[1][:].indirect(offsets(list_b, 0)), half(picked_a, 0), ALU.subtract)
+        nc.vector.tensor_tensor(gap[1][:], picked_b1[:], half(picked_a, 1), ALU.subtract)
+
+        ratio = [tile("ratio%d" % h, [P, HALF]) for h in range(2)]
+        capped = tile("capped", [P, SLOTS])
+        for h in range(2):
+            nc.scalar.activation(ratio[h][:], gap[h][:], ACT.Exp)
+            nc.vector.tensor_scalar(half(capped, h), ratio[h][:], CAP, None, ALU.min)
+        excess = tile("excess", [P, SLOTS])
+        base = tile("base", [P, SLOTS])
+        base_lam = tile("base_lam", [P, SLOTS])
+        for h in range(2):
+            nc.vector.tensor_scalar(half(excess, h), gap[h][:], LOG_CAP, 0.0, ALU.subtract, ALU.max)
+        nc.vector.tensor_tensor(base[:], excess[:], picked_a[:], ALU.add)
+        nc.vector.tensor_scalar(base_lam[:], base[:], lam_sb[:], None, ALU.mult)
+
+        soft = [tile("soft%d" % c, [P, 2, QUARTER]) for c in range(2)]
+        score = [tile("score%d" % c, [P, 2, QUARTER]) for c in range(2)]
+        top = [tile("top%d" % c, [P, 2, QUARTER // RUN]) for c in range(2)]
+        shifted = tile("shifted", [P, SLOTS])
+        for c in range(2):
+            nc.scalar.activation(soft[c][:], cross(capped, c), ACT.Ln, bias=1.0)
+        for c in range(2):
+            nc.vector.scalar_tensor_tensor(score[c][:], soft[c][:], lam_sb[:], cross(base_lam, c), ALU.mult, ALU.add)
+        for c in range(2):
+            nc.vector.tensor_reduce(
+                top[c][:], score[c][:].rearrange("p h (g e) -> p h g e", e=RUN), AX.X, ALU.max
+            )
+        for c in range(2):
+            nc.vector.tensor_tensor(
+                cross(shifted, c).rearrange("p h (g e) -> p h g e", e=RUN),
+                score[c][:].rearrange("p h (g e) -> p h g e", e=RUN),
+                top[c][:].unsqueeze(3).to_broadcast([P, 2, QUARTER // RUN, RUN]),
+                ALU.subtract,
+            )
+
+        run_sum = [tile("run_sum%d" % h, [P, HALF // RUN]) for h in range(2)]
+        others = [tile("others%d" % h, [P, HALF]) for h in range(2)]
+        others_sq = tile("others_sq", [P, SLOTS])
+        for h in range(2):
+            nc.scalar.activation(half(prob, h), half(shifted, h), ACT.Exp)
+        for h in range(2):
+            nc.vector.tensor_reduce(run_sum[h][:], runs(half(prob, h)), AX.X, ALU.add)
+        for h in range(2):
+            nc.vector.tensor_tensor(
+                runs(others[h][:]),
+                run_sum[h][:].unsqueeze(2).to_broadcast([P, HALF // RUN, RUN]),
+                runs(half(prob, h)),
+                ALU.subtract,
+            )
+        for h in range(2):
+            nc.vector.tensor_tensor(half(others_sq, h), others[h][:], others[h][:], ALU.mult)
+
+        inverse = tile("inverse", [P, SLOTS + 1])
+        odds = tile("odds", [P, SLOTS + 1])
+        total = tile("total", [P, 1])
+        nc.vector.memset(inverse[:, SLOTS : SLOTS + 1], 1.0)
+        nc.scalar.activation(inverse[:, 0:SLOTS], others_sq[:], ACT.Abs_reciprocal_sqrt)
+        nc.vector.scalar_tensor_tensor(odds[:], inverse[:], 1.0, prob[:], ALU.mult, ALU.mult, accum_out=total[:])
+        inv_total = tile("inv_total", [P, 1])
+        weights = tile("weights", [P, SLOTS])
+        nc.vector.reciprocal(inv_total[:], total[:])
+        nc.vector.tensor_scalar(weights[:], odds[:, 0:SLOTS], inv_total[:], 256.0, ALU.mult, ALU.mult)
+        nc.vector.tensor_copy(placed[:].indirect(list_a[:]), weights[:])
+
+        n0 = 0
+        for i, width in enumerate(OUT_PIECES):
+            piece = tile("piece%d" % i, [P, width])
+            cols = slice(n0, n0 + width)
+            nc.vector.scalar_tensor_tensor(piece[:], old_sb[:, cols], fade_sb[:], placed[:, cols], ALU.mult, ALU.add)
+            queue = nc.sync if i % 2 == 0 else nc.scalar
+            queue.dma_start(out=out[:, cols], in_=piece[:])
+            n0 = n0 + width

@@ -22,12 +22,11 @@ P = 128
 PACK = 4
 PASS_N = 256
 HALF = SLOTS // 2
-QUARTER = SLOTS // 4
 LIST_COLS = SLOTS // 16
 CAP_BITS = 60
 CAP = 2.0**CAP_BITS
 LOG_CAP = CAP_BITS * math.log(2.0)
-OUT_PIECES = [384, 384, 256]
+OUT_PIECES = [256, 256, 256, 256]
 
 
 def tile_attend_eithertoken_oddsof_counts_heads_kernel(
@@ -44,43 +43,31 @@ def tile_attend_eithertoken_oddsof_counts_heads_kernel(
         def half(t, h):
             return t[:, h * HALF : (h + 1) * HALF]
 
-        def cross(t, c):
-            return t[:].rearrange("p (h c n) -> p h c n", h=2, c=2)[:, :, c, :]
-
         def runs(ap):
             return ap.rearrange("p (g e) -> p g e", e=RUN)
 
         key_scales = tile("key_scales", [P, T], U8)
-        nc.vector.memset(key_scales[:].bitcast(I32), 0)
-        for quad in range(4):
-            nc.scalar.dma_start(
-                out=key_scales[32 * quad : 32 * quad + 4, :].bitcast(I32),
-                in_=keys_scales[0, 4 * quad : 4 * quad + 4, :].bitcast(I32),
-            )
+        nc.gpsimd.memset(key_scales[:].bitcast(I32), 0)
         q_raw = [tile("q_raw%d" % i, [P, PACK, Q]) for i in range(2)]
         key_words = tile("key_words", [P, 2 * T], U8)
         nc.sync.dma_start(out=q_raw[0][:], in_=query.rearrange("(p j) w -> p j w", j=PACK))
+        for quad in range(4):
+            nc.sync.dma_start(
+                out=key_scales[32 * quad : 32 * quad + 4, :].bitcast(I32),
+                in_=keys_scales[0, 4 * quad : 4 * quad + 4, :].bitcast(I32),
+            )
         nc.sync.dma_start(out=key_words[:].bitcast(I32), in_=keys_words[0].bitcast(I32))
         nc.sync.dma_start(out=q_raw[1][:], in_=query2.rearrange("(p j) w -> p j w", j=PACK))
         list_a = pool.tile([P, LIST_COLS], U16, name="list_a")
         list_b = pool.tile([P, LIST_COLS], U16, name="list_b")
         nc.sync.dma_start(list_a[:], offs)
         nc.sync.dma_start(list_b[:], offs2)
-        lam_sb = tile("lam_sb", [P, 1])
-        prob = tile("prob", [P, SLOTS + 1])
-        fade_sb = tile("fade_sb", [P, 1])
-        nc.sync.dma_start(out=lam_sb[:], in_=lam)
-        nc.sync.dma_start(out=prob[:, SLOTS : SLOTS + 1], in_=reserve)
-        nc.sync.dma_start(out=fade_sb[:], in_=fade)
-        old_sb = tile("old_sb", [P, T])
-        nc.sync.dma_start(out=old_sb[:], in_=old)
-
         placed = tile("placed", [P, T])
         nc.gpsimd.memset(placed[:], 0.0)
 
         scores = [tile("scores%d" % i, [P, T]) for i in range(2)]
         for i in range(2):
-            grouped = tile("grouped%d" % i, [P, Q, PACK], BF16)
+            grouped = tile("grouped", [P, Q, PACK], BF16)
             codes = tile("codes%d" % i, [P, Q], U32)
             q_scales = tile("q_scales%d" % i, [P, Q], U8)
             nc.vector.tensor_copy(out=grouped[:], in_=q_raw[i][:].rearrange("p j w -> p w j"))
@@ -98,49 +85,60 @@ def tile_attend_eithertoken_oddsof_counts_heads_kernel(
                     start=True,
                     stop=True,
                 )
-                nc.scalar.copy(out=scores[i][:, n0 : n0 + PASS_N], in_=bank[:])
+                if i == 0 and n0 == T - PASS_N:
+                    nc.vector.tensor_copy(out=scores[i][:, n0 : n0 + PASS_N], in_=bank[:])
+                else:
+                    nc.scalar.copy(out=scores[i][:, n0 : n0 + PASS_N], in_=bank[:])
+
+        old_sb = tile("q_raw0", [P, T])
+        nc.sync.dma_start(out=old_sb[:], in_=old)
+        late = tile("q_raw1", [P, SLOTS + 24])
+        prob = late[:, 0 : SLOTS + 1]
+        lam_sb = late[:, SLOTS + 8 : SLOTS + 9]
+        fade_sb = late[:, SLOTS + 16 : SLOTS + 17]
+        nc.sync.dma_start(out=lam_sb, in_=lam)
+        nc.sync.dma_start(out=prob[:, SLOTS : SLOTS + 1], in_=reserve)
+        nc.sync.dma_start(out=fade_sb, in_=fade)
 
         def offsets(lst, h):
             return lst[:, h * LIST_COLS // 2 : (h + 1) * LIST_COLS // 2]
 
         picked_a = tile("picked_a", [P, SLOTS])
-        nc.vector.tensor_copy(picked_a[:], scores[0][:].indirect(list_a[:]))
-        gap = [tile("gap%d" % h, [P, HALF]) for h in range(2)]
+        for h in range(2):
+            nc.vector.tensor_copy(half(picked_a, h), scores[0][:].indirect(offsets(list_a, h)))
+        gap = tile("gap", [P, SLOTS])
         picked_b1 = tile("picked_b1", [P, HALF])
         nc.scalar.activation(picked_b1[:], scores[1][:].indirect(offsets(list_b, 1)), ACT.Copy)
-        nc.vector.tensor_tensor(gap[0][:], scores[1][:].indirect(offsets(list_b, 0)), half(picked_a, 0), ALU.subtract)
-        nc.vector.tensor_tensor(gap[1][:], picked_b1[:], half(picked_a, 1), ALU.subtract)
+        nc.vector.tensor_tensor(half(gap, 0), scores[1][:].indirect(offsets(list_b, 0)), half(picked_a, 0), ALU.subtract)
+        nc.vector.tensor_tensor(half(gap, 1), picked_b1[:], half(picked_a, 1), ALU.subtract)
 
-        ratio = [tile("ratio%d" % h, [P, HALF]) for h in range(2)]
+        ratio = tile("ratio", [P, SLOTS])
         capped = tile("capped", [P, SLOTS])
         for h in range(2):
-            nc.scalar.activation(ratio[h][:], gap[h][:], ACT.Exp)
-            nc.vector.tensor_scalar(half(capped, h), ratio[h][:], CAP, None, ALU.min)
+            nc.scalar.activation(half(ratio, h), half(gap, h), ACT.Exp)
+        nc.vector.tensor_scalar(capped[:], ratio[:], CAP, None, ALU.min)
         excess = tile("excess", [P, SLOTS])
         base = tile("base", [P, SLOTS])
         base_lam = tile("base_lam", [P, SLOTS])
-        for h in range(2):
-            nc.vector.tensor_scalar(half(excess, h), gap[h][:], LOG_CAP, 0.0, ALU.subtract, ALU.max)
+        nc.vector.tensor_scalar(excess[:], gap[:], LOG_CAP, 0.0, ALU.subtract, ALU.max)
         nc.vector.tensor_tensor(base[:], excess[:], picked_a[:], ALU.add)
-        nc.vector.tensor_scalar(base_lam[:], base[:], lam_sb[:], None, ALU.mult)
+        nc.vector.tensor_scalar(base_lam[:], base[:], lam_sb, None, ALU.mult)
 
-        soft = [tile("soft%d" % c, [P, 2, QUARTER]) for c in range(2)]
-        score = [tile("score%d" % c, [P, 2, QUARTER]) for c in range(2)]
-        top = [tile("top%d" % c, [P, 2, QUARTER // RUN]) for c in range(2)]
-        shifted = tile("shifted", [P, SLOTS])
-        for c in range(2):
-            nc.scalar.activation(soft[c][:], cross(capped, c), ACT.Ln, bias=1.0)
-        for c in range(2):
-            nc.vector.scalar_tensor_tensor(score[c][:], soft[c][:], lam_sb[:], cross(base_lam, c), ALU.mult, ALU.add)
-        for c in range(2):
-            nc.vector.tensor_reduce(
-                top[c][:], score[c][:].rearrange("p h (g e) -> p h g e", e=RUN), AX.X, ALU.max
-            )
-        for c in range(2):
+        soft = [tile("soft%d" % h, [P, HALF]) for h in range(2)]
+        score = [tile("score%d" % h, [P, HALF]) for h in range(2)]
+        top = [tile("top%d" % h, [P, HALF // RUN]) for h in range(2)]
+        shifted = [tile("shifted%d" % h, [P, HALF]) for h in range(2)]
+        for h in range(2):
+            nc.scalar.activation(soft[h][:], half(capped, h), ACT.Ln, bias=1.0)
+        for h in range(2):
+            nc.vector.scalar_tensor_tensor(score[h][:], soft[h][:], lam_sb, half(base_lam, h), ALU.mult, ALU.add)
+        for h in range(2):
+            nc.vector.tensor_reduce(top[h][:], runs(score[h][:]), AX.X, ALU.max)
+        for h in range(2):
             nc.vector.tensor_tensor(
-                cross(shifted, c).rearrange("p h (g e) -> p h g e", e=RUN),
-                score[c][:].rearrange("p h (g e) -> p h g e", e=RUN),
-                top[c][:].unsqueeze(3).to_broadcast([P, 2, QUARTER // RUN, RUN]),
+                runs(shifted[h][:]),
+                runs(score[h][:]),
+                top[h][:].unsqueeze(2).to_broadcast([P, HALF // RUN, RUN]),
                 ALU.subtract,
             )
 
@@ -148,7 +146,7 @@ def tile_attend_eithertoken_oddsof_counts_heads_kernel(
         others = [tile("others%d" % h, [P, HALF]) for h in range(2)]
         others_sq = tile("others_sq", [P, SLOTS])
         for h in range(2):
-            nc.scalar.activation(half(prob, h), half(shifted, h), ACT.Exp)
+            nc.scalar.activation(half(prob, h), shifted[h][:], ACT.Exp)
         for h in range(2):
             nc.vector.tensor_reduce(run_sum[h][:], runs(half(prob, h)), AX.X, ALU.add)
         for h in range(2):
@@ -166,7 +164,7 @@ def tile_attend_eithertoken_oddsof_counts_heads_kernel(
         total = tile("total", [P, 1])
         nc.vector.memset(inverse[:, SLOTS : SLOTS + 1], 1.0)
         nc.scalar.activation(inverse[:, 0:SLOTS], others_sq[:], ACT.Abs_reciprocal_sqrt)
-        nc.vector.scalar_tensor_tensor(odds[:], inverse[:], 1.0, prob[:], ALU.mult, ALU.mult, accum_out=total[:])
+        nc.vector.scalar_tensor_tensor(odds[:], inverse[:], 1.0, prob, ALU.mult, ALU.mult, accum_out=total[:])
         inv_total = tile("inv_total", [P, 1])
         weights = tile("weights", [P, SLOTS])
         nc.vector.reciprocal(inv_total[:], total[:])
@@ -177,7 +175,7 @@ def tile_attend_eithertoken_oddsof_counts_heads_kernel(
         for i, width in enumerate(OUT_PIECES):
             piece = tile("piece%d" % i, [P, width])
             cols = slice(n0, n0 + width)
-            nc.vector.scalar_tensor_tensor(piece[:], old_sb[:, cols], fade_sb[:], placed[:, cols], ALU.mult, ALU.add)
+            nc.vector.scalar_tensor_tensor(piece[:], old_sb[:, cols], fade_sb, placed[:, cols], ALU.mult, ALU.add)
             queue = nc.sync if i % 2 == 0 else nc.scalar
             queue.dma_start(out=out[:, cols], in_=piece[:])
             n0 = n0 + width

@@ -51,13 +51,14 @@ def tile_attend_eithertoken_oddsof_counts_heads_kernel(
         q_raw = [tile("q_raw%d" % i, [P, PACK, Q]) for i in range(2)]
         key_words = tile("key_words", [P, 2 * T], U8)
         nc.sync.dma_start(out=q_raw[0][:], in_=query.rearrange("(p j) w -> p j w", j=PACK))
+        nc.sync.dma_start(out=key_words[:].bitcast(I32), in_=keys_words[0].bitcast(I32))
+        nc.sync.dma_start(out=q_raw[1][:], in_=query2.rearrange("(p j) w -> p j w", j=PACK))
         for quad in range(4):
-            nc.sync.dma_start(
+            queue = nc.sync if quad == 0 else nc.scalar
+            queue.dma_start(
                 out=key_scales[32 * quad : 32 * quad + 4, :].bitcast(I32),
                 in_=keys_scales[0, 4 * quad : 4 * quad + 4, :].bitcast(I32),
             )
-        nc.sync.dma_start(out=key_words[:].bitcast(I32), in_=keys_words[0].bitcast(I32))
-        nc.sync.dma_start(out=q_raw[1][:], in_=query2.rearrange("(p j) w -> p j w", j=PACK))
         list_a = pool.tile([P, LIST_COLS], U16, name="list_a")
         list_b = pool.tile([P, LIST_COLS], U16, name="list_b")
         nc.sync.dma_start(list_a[:], offs)
@@ -67,7 +68,7 @@ def tile_attend_eithertoken_oddsof_counts_heads_kernel(
 
         scores = [tile("scores%d" % i, [P, T]) for i in range(2)]
         for i in range(2):
-            grouped = tile("grouped", [P, Q, PACK], BF16)
+            grouped = tile("grouped%d" % i, [P, Q, PACK], BF16)
             codes = tile("codes%d" % i, [P, Q], U32)
             q_scales = tile("q_scales%d" % i, [P, Q], U8)
             nc.vector.tensor_copy(out=grouped[:], in_=q_raw[i][:].rearrange("p j w -> p w j"))

import math
from contextlib import ExitStack

import concourse.mybir as mybir

D, T, SLOTS, Q, RUN = 512, 1024, 512, 128, 8
FLOPS = 2 * 2 * D * Q * T

F32 = mybir.dt.float32
BF16 = mybir.dt.bfloat16
I32 = mybir.dt.int32
U32 = mybir.dt.uint32
U16 = mybir.dt.uint16
U8 = mybir.dt.uint8
FP8X4 = mybir.dt.float8_e4m3fn_x4
FP4X4 = mybir.dt.float4_e2m1fn_x4
ALU = mybir.AluOpType
ACT = mybir.ActivationFunctionType
AX = mybir.AxisListType

P = 128
PACK = 4
PASS_N = 256
HALF = SLOTS // 2
LIST_COLS = SLOTS // 16
CAP_BITS = 60
CAP = 2.0**CAP_BITS
LOG_CAP = CAP_BITS * math.log(2.0)
OUT_PIECES = [256, 256, 256, 256]


def tile_attend_eithertoken_oddsof_counts_heads_kernel(
    tc, query, query2, keys_words, keys_scales, lam, reserve, old, fade, offs, offs2, out
):
    nc = tc.nc
    with ExitStack() as ctx:
        pool = ctx.enter_context(tc.tile_pool(name="pool", bufs=1))
        psum = ctx.enter_context(tc.psum_pool(name="psum", bufs=1))

        def tile(name, shape, dtype=F32):
            return pool.tile(shape, dtype, name=name, align_bytes=64)

        def half(t, h):
            return t[:, h * HALF : (h + 1) * HALF]

        def runs(ap):
            return ap.rearrange("p (g e) -> p g e", e=RUN)

        key_scales = tile("key_scales", [P, T], U8)
        nc.gpsimd.memset(key_scales[:].bitcast(I32), 0)
        q_raw = [tile("q_raw%d" % i, [P, PACK, Q]) for i in range(2)]
        key_words = tile("key_words", [P, 2 * T], U8)
        nc.sync.dma_start(out=q_raw[0][:], in_=query.rearrange("(p j) w -> p j w", j=PACK))
        nc.sync.dma_start(out=key_words[:].bitcast(I32), in_=keys_words[0].bitcast(I32))
        nc.sync.dma_start(out=q_raw[1][:], in_=query2.rearrange("(p j) w -> p j w", j=PACK))
        for quad in range(4):
            queue = nc.sync if quad == 0 else nc.scalar
            queue.dma_start(
                out=key_scales[32 * quad : 32 * quad + 4, :].bitcast(I32),
                in_=keys_scales[0, 4 * quad : 4 * quad + 4, :].bitcast(I32),
            )
        list_a = pool.tile([P, LIST_COLS], U16, name="list_a")
        list_b = pool.tile([P, LIST_COLS], U16, name="list_b")
        nc.sync.dma_start(list_a[:], offs)
        nc.sync.dma_start(list_b[:], offs2)
        placed = tile("placed", [P, T])
        nc.gpsimd.memset(placed[:], 0.0)

        scores = [tile("scores%d" % i, [P, T]) for i in range(2)]
        for i in range(2):
            grouped = tile("grouped%d" % i, [P, Q, PACK], BF16)
            codes = tile("codes%d" % i, [P, Q], U32)
            q_scales = tile("q_scales%d" % i, [P, Q], U8)
            nc.vector.tensor_copy(out=grouped[:], in_=q_raw[i][:].rearrange("p j w -> p w j"))
            nc.vector.quantize_mx(
                out=codes[:].bitcast(FP8X4), scales=q_scales[:], in_=grouped[:].rearrange("p w j -> p (w j)")
            )
            for n0 in range(0, T, PASS_N):
                bank = psum.tile([Q, PASS_N], F32, name="bank%d_%d" % (i, n0))
                nc.tensor.matmul_mx(
                    out=bank[:],
                    lhsT=codes[:].bitcast(FP8X4),
                    lhsT_scale=q_scales[:],
                    rhs=key_words[:, 2 * n0 : 2 * (n0 + PASS_N)].bitcast(FP4X4),
                    rhs_scale=key_scales[:, n0 : n0 + PASS_N],
                    start=True,
                    stop=True,
                )
                if i == 0 and n0 == T - PASS_N:
                    nc.vector.tensor_copy(out=scores[i][:, n0 : n0 + PASS_N], in_=bank[:])
                else:
                    nc.scalar.copy(out=scores[i][:, n0 : n0 + PASS_N], in_=bank[:])

        old_sb = tile("q_raw0", [P, T])
        nc.sync.dma_start(out=old_sb[:], in_=old)
        late = tile("q_raw1", [P, SLOTS + 24])
        prob = late[:, 0 : SLOTS + 1]
        lam_sb = late[:, SLOTS + 8 : SLOTS + 9]
        fade_sb = late[:, SLOTS + 16 : SLOTS + 17]
        nc.sync.dma_start(out=lam_sb, in_=lam)
        nc.sync.dma_start(out=prob[:, SLOTS : SLOTS + 1], in_=reserve)
        nc.sync.dma_start(out=fade_sb, in_=fade)

        def offsets(lst, h):
            return lst[:, h * LIST_COLS // 2 : (h + 1) * LIST_COLS // 2]

        picked_a = tile("picked_a", [P, SLOTS])
        for h in range(2):
            nc.vector.tensor_copy(half(picked_a, h), scores[0][:].indirect(offsets(list_a, h)))
        gap = tile("gap", [P, SLOTS])
        picked_b1 = tile("picked_b1", [P, HALF])
        nc.scalar.activation(picked_b1[:], scores[1][:].indirect(offsets(list_b, 1)), ACT.Copy)
        nc.vector.tensor_tensor(half(gap, 0), scores[1][:].indirect(offsets(list_b, 0)), half(picked_a, 0), ALU.subtract)
        nc.vector.tensor_tensor(half(gap, 1), picked_b1[:], half(picked_a, 1), ALU.subtract)

        ratio = tile("ratio", [P, SLOTS])
        capped = tile("capped", [P, SLOTS])
        for h in range(2):
            nc.scalar.activation(half(ratio, h), half(gap, h), ACT.Exp)
        nc.vector.tensor_scalar(capped[:], ratio[:], CAP, None, ALU.min)
        excess = tile("excess", [P, SLOTS])
        base = tile("base", [P, SLOTS])
        base_lam = tile("base_lam", [P, SLOTS])
        nc.vector.tensor_scalar(excess[:], gap[:], LOG_CAP, 0.0, ALU.subtract, ALU.max)
        nc.vector.tensor_tensor(base[:], excess[:], picked_a[:], ALU.add)
        nc.vector.tensor_scalar(base_lam[:], base[:], lam_sb, None, ALU.mult)

        soft = [tile("soft%d" % h, [P, HALF]) for h in range(2)]
        score = [tile("score%d" % h, [P, HALF]) for h in range(2)]
        top = [tile("top%d" % h, [P, HALF // RUN]) for h in range(2)]
        shifted = [tile("shifted%d" % h, [P, HALF]) for h in range(2)]
        for h in range(2):
            nc.scalar.activation(soft[h][:], half(capped, h), ACT.Ln, bias=1.0)
        for h in range(2):
            nc.vector.scalar_tensor_tensor(score[h][:], soft[h][:], lam_sb, half(base_lam, h), ALU.mult, ALU.add)
        for h in range(2):
            nc.vector.tensor_reduce(top[h][:], runs(score[h][:]), AX.X, ALU.max)
        for h in range(2):
            nc.vector.tensor_tensor(
                runs(shifted[h][:]),
                runs(score[h][:]),
                top[h][:].unsqueeze(2).to_broadcast([P, HALF // RUN, RUN]),
                ALU.subtract,
            )

        run_sum = [tile("run_sum%d" % h, [P, HALF // RUN]) for h in range(2)]
        others = [tile("others%d" % h, [P, HALF]) for h in range(2)]
        others_sq = tile("others_sq", [P, SLOTS])
        for h in range(2):
            nc.scalar.activation(half(prob, h), shifted[h][:], ACT.Exp)
        for h in range(2):
            nc.vector.tensor_reduce(run_sum[h][:], runs(half(prob, h)), AX.X, ALU.add)
        for h in range(2):
            nc.vector.tensor_tensor(
                runs(others[h][:]),
                run_sum[h][:].unsqueeze(2).to_broadcast([P, HALF // RUN, RUN]),
                runs(half(prob, h)),
                ALU.subtract,
            )
        for h in range(2):
            nc.vector.tensor_tensor(half(others_sq, h), others[h][:], others[h][:], ALU.mult)

        inverse = tile("inverse", [P, SLOTS + 1])
        odds = tile("odds", [P, SLOTS + 1])
        total = tile("total", [P, 1])
        nc.vector.memset(inverse[:, SLOTS : SLOTS + 1], 1.0)
        nc.scalar.activation(inverse[:, 0:SLOTS], others_sq[:], ACT.Abs_reciprocal_sqrt)
        nc.vector.scalar_tensor_tensor(odds[:], inverse[:], 1.0, prob, ALU.mult, ALU.mult, accum_out=total[:])
        inv_total = tile("inv_total", [P, 1])
        weights = tile("weights", [P, SLOTS])
        nc.vector.reciprocal(inv_total[:], total[:])
        nc.vector.tensor_scalar(weights[:], odds[:, 0:SLOTS], inv_total[:], 256.0, ALU.mult, ALU.mult)
        nc.vector.tensor_copy(placed[:].indirect(list_a[:]), weights[:])

        n0 = 0
        for i, width in enumerate(OUT_PIECES):
            piece = tile("piece%d" % i, [P, width])
            cols = slice(n0, n0 + width)
            nc.vector.scalar_tensor_tensor(piece[:], old_sb[:, cols], fade_sb, placed[:, cols], ALU.mult, ALU.add)
            queue = nc.sync if i % 2 == 0 else nc.scalar
            queue.dma_start(out=out[:, cols], in_=piece[:])
            n0 = n0 + width
